import numpy as np
import ml_dtypes


def mxq(x, axis, fmt="e4m3"):
    dtype, down = {"e4m3": (ml_dtypes.float8_e4m3fn, 7), "e5m2": (ml_dtypes.float8_e5m2, 14)}[fmt]
    v = np.moveaxis(np.asarray(x, np.float32).astype(ml_dtypes.bfloat16).astype(np.float64), axis, -1)
    blocks = v.reshape(v.shape[:-1] + (-1, 32))
    amax = np.abs(blocks).max(-1, keepdims=True)
    byte = np.maximum(np.where(amax > 0, np.frexp(amax)[1] - 1 + 127, 0) - down, 1)
    scale = np.exp2(byte - 127.0)
    codes = (blocks / scale).astype(np.float32).astype(dtype).astype(np.float64)
    return np.moveaxis((codes * scale).reshape(v.shape), -1, axis)


WIDE = False


def mx_kscale(k):
    if not WIDE:
        return np.ones(k)
    levels = np.array([10, -10, 5, -5, 0])
    if k % 512:
        return np.exp2(np.random.permutation(np.resize(levels, k // 32))).repeat(32)
    a = np.empty((k // 512, 16))
    for p in range(k // 512):
        a[p, :8] = np.random.permutation(np.resize(levels, 8))
        for g in range(8):
            far = levels[np.abs(levels - a[p, g]) >= 10]
            a[p, g + 8] = far[np.random.randint(len(far))]
    return np.exp2(a.ravel()).repeat(32)


def f64(x):
    return np.asarray(x).astype(np.float64)


def striped(idx):
    return np.tile(idx.reshape(-1, 16).T, (8, 1)).astype(np.uint16)


def unstriped(offs):
    return offs[:16].T.reshape(-1).astype(np.int64)


def pack_weight(w):
    k, n = w.shape
    w = f64(np.asarray(w, np.float32).astype(ml_dtypes.bfloat16)).reshape(k // 32, 32, n)
    amax = np.abs(w).max(1)
    byte = np.clip(np.where(amax > 0, np.frexp(amax)[1] - 1 + 127 - 7, 1), 1, 254)
    scaled = (w * np.exp2(127.0 - byte)[:, None, :]).reshape(k, n).astype(np.float32)
    words = np.ascontiguousarray(scaled.reshape(k // 512, 128, 4, n).transpose(0, 1, 3, 2)).astype(ml_dtypes.float8_e4m3fn).view(np.uint8)
    return words, np.ascontiguousarray(byte.astype(np.uint8).reshape(k // 512, 16, n))


def unpack_weight(words, scales):
    g, p, n, _ = words.shape
    vals = np.ascontiguousarray(words).view(ml_dtypes.float8_e4m3fn).astype(np.float64) * np.repeat(np.exp2(scales.astype(np.float64) - 127.0), 8, axis=1)[..., None]
    return vals.transpose(0, 1, 3, 2).reshape(g * 512, n)


def sigmoid(v):
    return 1.0 / (1.0 + np.exp(-np.maximum(v, -700.0)))


K, T, S, D, N = 1024, 2048, 512, 4, 256


def setup_inputs():
    n = np.random.standard_normal
    s = mx_kscale(K)[:, None]
    packed_xT = pack_weight(n((K, T)) * s)
    return {
        "x_words": packed_xT[0],
        "x_scales": packed_xT[1],
        "w1": (n((K, N)) / np.sqrt(K) / s).astype(np.float32),
        "w2": (n((K, N)) / np.sqrt(K) / s).astype(np.float32),
        "offs": striped(np.random.permutation(T)[:S]),
        "away": striped(np.random.permutation(T)[:S]),
    }


def reference(x_words, x_scales, w1, w2, offs, away):
    xq = unpack_weight(x_words, x_scales)[:, unstriped(offs)]
    w2q = mxq(f64(w2), 0, "e4m3")
    s1 = np.exp(0.5 * (w2q.T @ xq))
    w1q = mxq(f64(w1), 0, "e4m3")
    y1 = w1q.T @ xq
    x_away = unpack_weight(x_words, x_scales)[:, unstriped(away)]
    y2 = w1q.T @ x_away
    s2 = np.exp(0.5 * (w2q.T @ x_away))
    sc = np.sqrt(s1.reshape(len(s1), -1, D).sum(axis=2) + s2.reshape(len(s2), -1, D).sum(axis=2) + 1.0)
    t0 = (y1.reshape(len(y1), -1, D).sum(axis=2) - (y2.reshape(len(y2), -1, D).sum(axis=2))) / sc
    vv = (0.3989 * (np.exp(-0.5 * ((t0) ** 2)))) / (sigmoid(1.702 * t0) + 0.02)
    return s1 - (((s1) ** 2) * (np.repeat((vv * (vv + t0)) / ((sc) ** 2), D, axis=1)))

@@ -1,0 +1,211 @@
+import math
+from contextlib import ExitStack
+
+import concourse.mybir as mybir
+
+K, T, S, D, N = 1024, 2048, 512, 4, 256
+P = 128
+PACK = 4
+K_PASS = P * PACK
+PASSES = K // K_PASS
+BLOCKS = N // P
+TEAMS = S // D
+HALF = S // 2
+
+F32 = mybir.dt.float32
+BF16 = mybir.dt.bfloat16
+I32 = mybir.dt.int32
+U32 = mybir.dt.uint32
+U16 = mybir.dt.uint16
+U8 = mybir.dt.uint8
+FP8X4 = mybir.dt.float8_e4m3fn_x4
+ACT = mybir.ActivationFunctionType
+ALU = mybir.AluOpType
+AXIS = mybir.AxisListType
+
+FLOPS = 4 * 2 * K * N * S
+
+PDF = 0.3989
+SLOPE = 1.702
+FLOOR = 0.02
+TANH_SHIFT = 0.5 * math.log((1.0 + FLOOR) / FLOOR)
+TANH_TOP = 1.0 + 2.0 * FLOOR
+GAIN = PDF / (2.0 * FLOOR * (1.0 + FLOOR))
+
+
+def tile_picked_yskill_var_p_kernel(tc, x_words, x_scales, w1, w2, offs, away, out):
+    nc = tc.nc
+    with ExitStack() as ctx:
+        held = ctx.enter_context(tc.tile_pool(name="held", bufs=1))
+        psum = ctx.enter_context(tc.psum_pool(name="psum", bufs=1))
+
+        lists = []
+        for side, src in enumerate((offs, away)):
+            offsets = held.tile([P, S // 16], U16, name=f"offsets{side}")
+            nc.sync.dma_start(offsets[:], src)
+            lists.append(offsets)
+
+        scale_table = held.tile([P, T], U8, name="scale_table", align_bytes=64)
+        nc.vector.memset(scale_table[:].bitcast(I32), 0)
+        for q in range(4):
+            nc.sync.dma_start(
+                out=scale_table[32 * q : 32 * q + 4 * PASSES, :].bitcast(I32),
+                in_=x_scales[:, 4 * q : 4 * q + 4, :].bitcast(I32),
+            )
+
+        def load_words(g):
+            table = held.tile([P, T], I32, name=f"word_table{g}", align_bytes=64)
+            nc.sync.dma_start(out=table[:], in_=x_words[g].rearrange("p n t -> p (n t)").bitcast(I32))
+            return table
+
+        def load_weight(w, name, g):
+            raw = held.tile([P, PACK, N], F32, name=f"{name}_raw{g}", align_bytes=64)
+            nc.sync.dma_start(out=raw[:], in_=w[g * K_PASS : (g + 1) * K_PASS, :].rearrange("(p j) n -> p j n", j=PACK))
+            return raw
+
+        word_tables = [load_words(0)]
+        w2_raw = [load_weight(w2, "w2", g) for g in range(PASSES)]
+        word_tables.append(load_words(1))
+        w1_raw = [load_weight(w1, "w1", g) for g in range(PASSES)]
+
+        picked_scales = []
+        for side in range(2):
+            picked = held.tile([P, S], U8, name=f"picked_scales{side}", align_bytes=64)
+            nc.vector.tensor_copy(picked[:], scale_table[:].indirect(lists[side][:]))
+            dealt = held.tile([P, S], U8, name=f"dealt_scales{side}", align_bytes=64)
+            nc.vector.tensor_copy(
+                dealt[:].rearrange("p (d v) -> p d v", d=D), picked[:].rearrange("p (v d) -> p d v", d=D)
+            )
+            picked_scales.append(dealt)
+
+        def gather_words(side, g, tag):
+            picked = held.tile([P, S], U32, name=f"picked_words{side}{g}", tag=tag, align_bytes=64)
+            nc.vector.tensor_copy(
+                picked[:].rearrange("p (d v) -> p v d", d=D), word_tables[g][:].bitcast(U32).indirect(lists[side][:])
+            )
+            return picked
+
+        def interleave(copy, raw, name):
+            grouped = held.tile([P, N, PACK], BF16, name=f"{name}_grouped", tag=f"{name}_grouped", align_bytes=64)
+            copy(
+                grouped[:].rearrange("p (c i) t -> p c t i", i=4),
+                raw[:].rearrange("p t (c i) -> p c t i", i=4),
+            )
+            return grouped
+
+        def quantize(grouped, name):
+            codes = held.tile([P, N], U32, name=f"{name}_codes", align_bytes=64)
+            scales = held.tile([P, N], U8, name=f"{name}_scales", align_bytes=64)
+            nc.vector.quantize_mx(
+                out=codes[:].bitcast(FP8X4), scales=scales[:], in_=grouped[:].rearrange("p n t -> p (n t)")
+            )
+            return codes, scales
+
+        def product(bank, weight, b, side, g, cols, start, stop):
+            codes, scales = weight
+            nc.tensor.matmul_mx(
+                out=bank,
+                lhsT=codes[:, b * P : (b + 1) * P].bitcast(FP8X4),
+                lhsT_scale=scales[:, b * P : (b + 1) * P],
+                rhs=picked_words[side][g][:, cols].bitcast(FP8X4),
+                rhs_scale=picked_scales[side][4 * g : P, cols],
+                start=start,
+                stop=stop,
+            )
+
+        z_banks = [[psum.tile([P, S], F32, name=f"z{b}{side}") for side in range(2)] for b in range(BLOCKS)]
+        picked_words = [[None] * PASSES for side in range(2)]
+        spread = [held.tile([P, BLOCKS, S], F32, name=f"spread{side}") for side in range(2)]
+
+        for side in range(2):
+            picked_words[side][0] = gather_words(side, 0, f"first{side}")
+        w2_q = [quantize(interleave(nc.scalar.copy, w2_raw[g], f"w2{g}"), f"w2{g}") for g in range(PASSES)]
+        for side in range(2):
+            for b in range(BLOCKS):
+                product(z_banks[b][side][:], w2_q[0], b, side, 0, slice(0, S), True, False)
+        for side in range(2):
+            picked_words[side][1] = gather_words(side, 1, f"w2{1 - side}_grouped")
+            for b in range(BLOCKS):
+                product(z_banks[b][side][:], w2_q[1], b, side, 1, slice(0, S), False, True)
+        w1_grouped = [
+            interleave((nc.scalar.copy, nc.vector.tensor_copy)[g], w1_raw[g], f"w1{g}") for g in range(PASSES)
+        ]
+        for side in range(2):
+            for b in range(BLOCKS):
+                nc.scalar.activation(
+                    spread[side][:, b, :].rearrange("p (v d) -> p v d", d=D),
+                    z_banks[b][side][:].rearrange("p (d v) -> p v d", d=D),
+                    ACT.Exp,
+                    scale=0.5,
+                )
+
+        w1_q = [quantize(w1_grouped[g], f"w1{g}") for g in range(PASSES)]
+        y_banks = [psum.tile([P, BLOCKS, TEAMS], F32, name=f"y{side}") for side in range(2)]
+        for side in (1, 0):
+            for b in range(BLOCKS):
+                for g in range(PASSES):
+                    for d in range(D):
+                        product(
+                            y_banks[side][:, b, :],
+                            w1_q[g],
+                            b,
+                            side,
+                            g,
+                            slice(d * TEAMS, (d + 1) * TEAMS),
+                            g == 0 and d == 0,
+                            g == PASSES - 1 and d == D - 1,
+                        )
+
+        team_spread = held.tile([P, 2, BLOCKS, TEAMS], F32, name="team_spread")
+        nc.vector.tensor_reduce(
+            team_spread[:, 0], spread[0][:].rearrange("p b (v d) -> p b v d", d=D), AXIS.X, ALU.add
+        )
+        for b in range(BLOCKS):
+            nc.vector.tensor_reduce(
+                team_spread[:, 1, b, :], spread[1][:, b, :].rearrange("p (v d) -> p v d", d=D), AXIS.X, ALU.add
+            )
+        total = held.tile([P, BLOCKS, TEAMS], F32, name="total")
+        nc.vector.tensor_tensor(total[:], team_spread[:, 0], team_spread[:, 1], ALU.add)
+        inv_sc = held.tile([P, BLOCKS, TEAMS], F32, name="inv_sc")
+        nc.scalar.activation(inv_sc[:], total[:], ACT.Abs_reciprocal_sqrt, bias=1.0)
+
+        lead = held.tile([P, BLOCKS, TEAMS], F32, name="lead")
+        losers_y = held.tile([P, BLOCKS, TEAMS], F32, name="losers_y")
+        nc.vector.tensor_copy(losers_y[:], y_banks[1][:])
+        nc.vector.tensor_tensor(lead[:], y_banks[0][:], losers_y[:], ALU.subtract)
+        t0 = held.tile([P, BLOCKS, TEAMS], F32, name="t0")
+        nc.vector.tensor_tensor(t0[:], lead[:], inv_sc[:], ALU.mult)
+        t0_sq = held.tile([P, BLOCKS, TEAMS], F32, name="t0_sq")
+        nc.vector.tensor_tensor(t0_sq[:], t0[:], t0[:], ALU.mult)
+        pull = held.tile([P, BLOCKS, TEAMS], F32, name="pull")
+        nc.vector.scalar_tensor_tensor(pull[:], t0[:], 1.0 / GAIN, inv_sc[:], ALU.mult, ALU.mult)
+
+        coef = []
+        for b in range(BLOCKS):
+            bell = held.tile([P, TEAMS], F32, name=f"bell{b}")
+            nc.scalar.activation(bell[:], t0_sq[:, b, :], ACT.Exp, scale=-0.5)
+            bend = held.tile([P, TEAMS], F32, name=f"bend{b}")
+            nc.scalar.activation(bend[:], t0[:, b, :], ACT.Tanh, scale=0.5 * SLOPE, bias=TANH_SHIFT)
+            bell_sc = held.tile([P, TEAMS], F32, name=f"bell_sc{b}")
+            nc.vector.tensor_tensor(bell_sc[:], bell[:], inv_sc[:, b, :], ALU.mult)
+            ratio = held.tile([P, TEAMS], F32, name=f"ratio{b}")
+            nc.vector.scalar_tensor_tensor(ratio[:], bend[:], TANH_TOP, bell_sc[:], ALU.subtract, ALU.mult)
+            gap = held.tile([P, TEAMS], F32, name=f"gap{b}")
+            nc.vector.tensor_tensor(gap[:], pull[:, b, :], ratio[:], ALU.subtract)
+            factor = held.tile([P, TEAMS], F32, name=f"factor{b}")
+            nc.vector.scalar_tensor_tensor(factor[:], gap[:], GAIN * GAIN, ratio[:], ALU.mult, ALU.mult)
+            coef.append(factor)
+
+        for b, j0, j1 in ((0, 0, S), (1, 0, HALF), (1, HALF, S)):
+            s1 = spread[0][:, b, j0:j1]
+            teams = coef[b][:, j0 // D : j1 // D]
+            change = held.tile([P, j1 - j0], F32, name=f"change{b}{j0}")
+            nc.vector.tensor_tensor(
+                change[:].rearrange("p (v d) -> p v d", d=D),
+                s1.rearrange("p (v d) -> p v d", d=D),
+                teams.unsqueeze(2).to_broadcast([P, (j1 - j0) // D, D]),
+                ALU.mult,
+            )
+            result = held.tile([P, j1 - j0], F32, name=f"result{b}{j0}")
+            nc.vector.scalar_tensor_tensor(result[:], change[:], 1.0, s1, ALU.add, ALU.mult)
+            nc.sync.dma_start(out=out[b * P : (b + 1) * P, j0:j1], in_=result[:])

@@ -37,6 +37,7 @@ def tile_picked_yskill_var_p_kernel(tc, x_words, x_scales, w1, w2, offs, away, o
     nc = tc.nc
     with ExitStack() as ctx:
         held = ctx.enter_context(tc.tile_pool(name="held", bufs=1))
+        reused = ctx.enter_context(tc.tile_pool(name="reused", bufs=1))
         psum = ctx.enter_context(tc.psum_pool(name="psum", bufs=1))
 
         lists = []
@@ -54,7 +55,7 @@ def tile_picked_yskill_var_p_kernel(tc, x_words, x_scales, w1, w2, offs, away, o
             )
 
         def load_words(g):
-            table = held.tile([P, T], I32, name=f"word_table{g}", align_bytes=64)
+            table = reused.tile([P, T], I32, name=f"word_table{g}", offset=g * T * 4, align_bytes=64)
             nc.sync.dma_start(out=table[:], in_=x_words[g].rearrange("p n t -> p (n t)").bitcast(I32))
             return table
 
@@ -78,23 +79,24 @@ def tile_picked_yskill_var_p_kernel(tc, x_words, x_scales, w1, w2, offs, away, o
             )
             picked_scales.append(dealt)
 
-        def gather_words(side, g, tag):
-            picked = held.tile([P, S], U32, name=f"picked_words{side}{g}", tag=tag, align_bytes=64)
+        def gather_words(side, g):
+            if g == 0:
+                picked = held.tile([P, S], U32, name=f"picked_words{side}{g}", align_bytes=64)
+            else:
+                picked = reused.tile([P, S], U32, name=f"picked_words{side}{g}", offset=16384 + side * 2048, align_bytes=64)
             nc.vector.tensor_copy(
                 picked[:].rearrange("p (d v) -> p v d", d=D), word_tables[g][:].bitcast(U32).indirect(lists[side][:])
             )
             return picked
 
-        def interleave(copy, raw, name):
-            grouped = held.tile([P, N, PACK], BF16, name=f"{name}_grouped", tag=f"{name}_grouped", align_bytes=64)
+        def interleave(copy, raw, grouped):
             copy(
                 grouped[:].rearrange("p (c i) t -> p c t i", i=4),
                 raw[:].rearrange("p t (c i) -> p c t i", i=4),
             )
             return grouped
 
-        def quantize(grouped, name):
-            codes = held.tile([P, N], U32, name=f"{name}_codes", align_bytes=64)
+        def quantize(grouped, codes, name):
             scales = held.tile([P, N], U8, name=f"{name}_scales", align_bytes=64)
             nc.vector.quantize_mx(
                 out=codes[:].bitcast(FP8X4), scales=scales[:], in_=grouped[:].rearrange("p n t -> p (n t)")
@@ -115,31 +117,41 @@ def tile_picked_yskill_var_p_kernel(tc, x_words, x_scales, w1, w2, offs, away, o
 
         z_banks = [[psum.tile([P, S], F32, name=f"z{b}{side}") for side in range(2)] for b in range(BLOCKS)]
         picked_words = [[None] * PASSES for side in range(2)]
-        spread = [held.tile([P, BLOCKS, S], F32, name=f"spread{side}") for side in range(2)]
+        spread = [held.tile([P, 2, S], F32, name=f"spread{b}") for b in range(BLOCKS)]
 
         for side in range(2):
-            picked_words[side][0] = gather_words(side, 0, f"first{side}")
-        w2_q = [quantize(interleave(nc.scalar.copy, w2_raw[g], f"w2{g}"), f"w2{g}") for g in range(PASSES)]
+            picked_words[side][0] = gather_words(side, 0)
+        w2_q = []
+        for g in range(PASSES):
+            grouped = reused.tile([P, N, PACK], BF16, name=f"w2{g}_grouped", offset=(20480, 17408)[g], align_bytes=64)
+            codes = held.tile([P, N], U32, name=f"w2{g}_codes", align_bytes=64)
+            w2_q.append(quantize(interleave(nc.scalar.copy, w2_raw[g], grouped), codes, f"w2{g}"))
         for side in range(2):
             for b in range(BLOCKS):
                 product(z_banks[b][side][:], w2_q[0], b, side, 0, slice(0, S), True, False)
         for side in range(2):
-            picked_words[side][1] = gather_words(side, 1, f"w2{1 - side}_grouped")
+            picked_words[side][1] = gather_words(side, 1)
             for b in range(BLOCKS):
                 product(z_banks[b][side][:], w2_q[1], b, side, 1, slice(0, S), False, True)
+        w1_first = held.tile([P, N, PACK], BF16, name="w1_first", align_bytes=64)
+        w1_second = reused.tile([P, N, PACK], BF16, name="w1_second", offset=T * 4, align_bytes=64)
         w1_grouped = [
-            interleave((nc.scalar.copy, nc.vector.tensor_copy)[g], w1_raw[g], f"w1{g}") for g in range(PASSES)
+            interleave(nc.scalar.copy, w1_raw[0], w1_first),
+            interleave(nc.vector.tensor_copy, w1_raw[1], w1_second),
         ]
         for side in range(2):
             for b in range(BLOCKS):
                 nc.scalar.activation(
-                    spread[side][:, b, :].rearrange("p (v d) -> p v d", d=D),
+                    spread[b][:, side, :].rearrange("p (v d) -> p v d", d=D),
                     z_banks[b][side][:].rearrange("p (d v) -> p v d", d=D),
                     ACT.Exp,
                     scale=0.5,
                 )
 
-        w1_q = [quantize(w1_grouped[g], f"w1{g}") for g in range(PASSES)]
+        w1_q = []
+        for g in range(PASSES):
+            codes = reused.tile([P, N], U32, name=f"w1{g}_codes", offset=T * 4 + 2048 + g * N * 4, align_bytes=64)
+            w1_q.append(quantize(w1_grouped[g], codes, f"w1{g}"))
         y_banks = [psum.tile([P, BLOCKS, TEAMS], F32, name=f"y{side}") for side in range(2)]
         for side in (1, 0):
             for b in range(BLOCKS):
@@ -156,23 +168,18 @@ def tile_picked_yskill_var_p_kernel(tc, x_words, x_scales, w1, w2, offs, away, o
                             g == PASSES - 1 and d == D - 1,
                         )
 
-        team_spread = held.tile([P, 2, BLOCKS, TEAMS], F32, name="team_spread")
-        nc.vector.tensor_reduce(
-            team_spread[:, 0], spread[0][:].rearrange("p b (v d) -> p b v d", d=D), AXIS.X, ALU.add
-        )
+        total = held.tile([P, BLOCKS, TEAMS], F32, name="total")
         for b in range(BLOCKS):
             nc.vector.tensor_reduce(
-                team_spread[:, 1, b, :], spread[1][:, b, :].rearrange("p (v d) -> p v d", d=D), AXIS.X, ALU.add
+                total[:, b, :], spread[b][:].rearrange("p l (v d) -> p v l d", d=D), AXIS.XY, ALU.add
             )
-        total = held.tile([P, BLOCKS, TEAMS], F32, name="total")
-        nc.vector.tensor_tensor(total[:], team_spread[:, 0], team_spread[:, 1], ALU.add)
         inv_sc = held.tile([P, BLOCKS, TEAMS], F32, name="inv_sc")
         nc.scalar.activation(inv_sc[:], total[:], ACT.Abs_reciprocal_sqrt, bias=1.0)
 
         lead = held.tile([P, BLOCKS, TEAMS], F32, name="lead")
-        losers_y = held.tile([P, BLOCKS, TEAMS], F32, name="losers_y")
-        nc.vector.tensor_copy(losers_y[:], y_banks[1][:])
-        nc.vector.tensor_tensor(lead[:], y_banks[0][:], losers_y[:], ALU.subtract)
+        losers_y = spread[BLOCKS - 1][:, 1, 0 : BLOCKS * TEAMS].rearrange("p (b v) -> p b v", b=BLOCKS)
+        nc.vector.tensor_copy(losers_y, y_banks[1][:])
+        nc.vector.tensor_tensor(lead[:], y_banks[0][:], losers_y, ALU.subtract)
         t0 = held.tile([P, BLOCKS, TEAMS], F32, name="t0")
         nc.vector.tensor_tensor(t0[:], lead[:], inv_sc[:], ALU.mult)
         t0_sq = held.tile([P, BLOCKS, TEAMS], F32, name="t0_sq")
@@ -197,7 +204,7 @@ def tile_picked_yskill_var_p_kernel(tc, x_words, x_scales, w1, w2, offs, away, o
             coef.append(factor)
 
         for b, j0, j1 in ((0, 0, S), (1, 0, HALF), (1, HALF, S)):
-            s1 = spread[0][:, b, j0:j1]
+            s1 = spread[b][:, 0, j0:j1]
             teams = coef[b][:, j0 // D : j1 // D]
             change = held.tile([P, j1 - j0], F32, name=f"change{b}{j0}")
             nc.vector.tensor_tensor(

@@ -178,25 +178,28 @@ def tile_picked_yskill_var_p_kernel(tc, x_words, x_scales, w1, w2, offs, away, o
 
         lead = held.tile([P, BLOCKS, TEAMS], F32, name="lead")
         losers_y = spread[BLOCKS - 1][:, 1, 0 : BLOCKS * TEAMS].rearrange("p (b v) -> p b v", b=BLOCKS)
-        nc.vector.tensor_copy(losers_y, y_banks[1][:])
-        nc.vector.tensor_tensor(lead[:], y_banks[0][:], losers_y, ALU.subtract)
         t0 = held.tile([P, BLOCKS, TEAMS], F32, name="t0")
-        nc.vector.tensor_tensor(t0[:], lead[:], inv_sc[:], ALU.mult)
         t0_sq = held.tile([P, BLOCKS, TEAMS], F32, name="t0_sq")
-        nc.vector.tensor_tensor(t0_sq[:], t0[:], t0[:], ALU.mult)
         pull = held.tile([P, BLOCKS, TEAMS], F32, name="pull")
+        for b in range(BLOCKS):
+            nc.vector.tensor_copy(losers_y[:, b, :], y_banks[1][:, b, :])
+        for b in range(BLOCKS):
+            nc.vector.tensor_tensor(lead[:, b, :], y_banks[0][:, b, :], losers_y[:, b, :], ALU.subtract)
+        for b in range(BLOCKS):
+            nc.vector.tensor_tensor(t0[:, b, :], lead[:, b, :], inv_sc[:, b, :], ALU.mult)
+        for b in range(BLOCKS):
+            nc.vector.tensor_tensor(t0_sq[:, b, :], t0[:, b, :], t0[:, b, :], ALU.mult)
         nc.vector.scalar_tensor_tensor(pull[:], t0[:], 1.0 / GAIN, inv_sc[:], ALU.mult, ALU.mult)
-
         coef = []
         for b in range(BLOCKS):
-            bell = held.tile([P, TEAMS], F32, name=f"bell{b}")
-            nc.scalar.activation(bell[:], t0_sq[:, b, :], ACT.Exp, scale=-0.5)
             bend = held.tile([P, TEAMS], F32, name=f"bend{b}")
             nc.scalar.activation(bend[:], t0[:, b, :], ACT.Tanh, scale=0.5 * SLOPE, bias=TANH_SHIFT)
-            bell_sc = held.tile([P, TEAMS], F32, name=f"bell_sc{b}")
-            nc.vector.tensor_tensor(bell_sc[:], bell[:], inv_sc[:, b, :], ALU.mult)
+            bell = held.tile([P, TEAMS], F32, name=f"bell{b}")
+            nc.scalar.activation(bell[:], t0_sq[:, b, :], ACT.Exp, scale=-0.5)
+            bend_sc = held.tile([P, TEAMS], F32, name=f"bend_sc{b}")
+            nc.vector.scalar_tensor_tensor(bend_sc[:], bend[:], TANH_TOP, inv_sc[:, b, :], ALU.subtract, ALU.mult)
             ratio = held.tile([P, TEAMS], F32, name=f"ratio{b}")
-            nc.vector.scalar_tensor_tensor(ratio[:], bend[:], TANH_TOP, bell_sc[:], ALU.subtract, ALU.mult)
+            nc.vector.tensor_tensor(ratio[:], bend_sc[:], bell[:], ALU.mult)
             gap = held.tile([P, TEAMS], F32, name=f"gap{b}")
             nc.vector.tensor_tensor(gap[:], pull[:, b, :], ratio[:], ALU.subtract)
             factor = held.tile([P, TEAMS], F32, name=f"factor{b}")

@@ -3,7 +3,11 @@ from contextlib import ExitStack
 
 import concourse.mybir as mybir
 
-K, T, S, D, N = 1024, 2048, 512, 4, 256
+K = 1024
+T = 2048
+S = 512
+D = 4
+N = 256
 P = 128
 PACK = 4
 K_PASS = P * PACK
@@ -11,6 +15,19 @@ PASSES = K // K_PASS
 BLOCKS = N // P
 TEAMS = S // D
 HALF = S // 2
+QUADRANT = 32
+SCALE_ROWS = 4
+RUN = 4
+WINNERS, LOSERS = 0, 1
+
+TABLE_BYTES = T * 4
+PICKED_BYTES = S * 4
+GROUPED_BYTES = N * PACK * 2
+CODE_BYTES = N * 4
+PICKED_AT = PASSES * TABLE_BYTES
+W2_GROUPED_AT = (PICKED_AT + 2 * PICKED_BYTES, PICKED_AT + PICKED_BYTES // 2)
+W1_GROUPED_AT = TABLE_BYTES
+W1_CODES_AT = W1_GROUPED_AT + GROUPED_BYTES
 
 F32 = mybir.dt.float32
 BF16 = mybir.dt.bfloat16
@@ -48,14 +65,14 @@ def tile_picked_yskill_var_p_kernel(tc, x_words, x_scales, w1, w2, offs, away, o
 
         scale_table = held.tile([P, T], U8, name="scale_table", align_bytes=64)
         nc.vector.memset(scale_table[:].bitcast(I32), 0)
-        for q in range(4):
+        for q in range(P // QUADRANT):
             nc.sync.dma_start(
-                out=scale_table[32 * q : 32 * q + 4 * PASSES, :].bitcast(I32),
-                in_=x_scales[:, 4 * q : 4 * q + 4, :].bitcast(I32),
+                out=scale_table[QUADRANT * q : QUADRANT * q + SCALE_ROWS * PASSES, :].bitcast(I32),
+                in_=x_scales[:, SCALE_ROWS * q : SCALE_ROWS * (q + 1), :].bitcast(I32),
             )
 
         def load_words(g):
-            table = reused.tile([P, T], I32, name=f"word_table{g}", offset=g * T * 4, align_bytes=64)
+            table = reused.tile([P, T], I32, name=f"word_table{g}", offset=g * TABLE_BYTES, align_bytes=64)
             nc.sync.dma_start(out=table[:], in_=x_words[g].rearrange("p n t -> p (n t)").bitcast(I32))
             return table
 
@@ -83,7 +100,8 @@ def tile_picked_yskill_var_p_kernel(tc, x_words, x_scales, w1, w2, offs, away, o
             if g == 0:
                 picked = held.tile([P, S], U32, name=f"picked_words{side}{g}", align_bytes=64)
             else:
-                picked = reused.tile([P, S], U32, name=f"picked_words{side}{g}", offset=16384 + side * 2048, align_bytes=64)
+                at = PICKED_AT + side * PICKED_BYTES
+                picked = reused.tile([P, S], U32, name=f"picked_words{side}{g}", offset=at, align_bytes=64)
             nc.vector.tensor_copy(
                 picked[:].rearrange("p (d v) -> p v d", d=D), word_tables[g][:].bitcast(U32).indirect(lists[side][:])
             )
@@ -91,8 +109,8 @@ def tile_picked_yskill_var_p_kernel(tc, x_words, x_scales, w1, w2, offs, away, o
 
         def interleave(copy, raw, grouped):
             copy(
-                grouped[:].rearrange("p (c i) t -> p c t i", i=4),
-                raw[:].rearrange("p t (c i) -> p c t i", i=4),
+                grouped[:].rearrange("p (c i) t -> p c t i", i=RUN),
+                raw[:].rearrange("p t (c i) -> p c t i", i=RUN),
             )
             return grouped
 
@@ -103,14 +121,14 @@ def tile_picked_yskill_var_p_kernel(tc, x_words, x_scales, w1, w2, offs, away, o
             )
             return codes, scales
 
-        def product(bank, weight, b, side, g, cols, start, stop):
-            codes, scales = weight
+        def product(bank, quantized, b, side, g, cols, start, stop):
+            codes, scales = quantized
             nc.tensor.matmul_mx(
                 out=bank,
                 lhsT=codes[:, b * P : (b + 1) * P].bitcast(FP8X4),
                 lhsT_scale=scales[:, b * P : (b + 1) * P],
                 rhs=picked_words[side][g][:, cols].bitcast(FP8X4),
-                rhs_scale=picked_scales[side][4 * g : P, cols],
+                rhs_scale=picked_scales[side][SCALE_ROWS * g : P, cols],
                 start=start,
                 stop=stop,
             )
@@ -123,7 +141,7 @@ def tile_picked_yskill_var_p_kernel(tc, x_words, x_scales, w1, w2, offs, away, o
             picked_words[side][0] = gather_words(side, 0)
         w2_q = []
         for g in range(PASSES):
-            grouped = reused.tile([P, N, PACK], BF16, name=f"w2{g}_grouped", offset=(20480, 17408)[g], align_bytes=64)
+            grouped = reused.tile([P, N, PACK], BF16, name=f"w2{g}_grouped", offset=W2_GROUPED_AT[g], align_bytes=64)
             codes = held.tile([P, N], U32, name=f"w2{g}_codes", align_bytes=64)
             w2_q.append(quantize(interleave(nc.scalar.copy, w2_raw[g], grouped), codes, f"w2{g}"))
         for side in range(2):
@@ -133,12 +151,14 @@ def tile_picked_yskill_var_p_kernel(tc, x_words, x_scales, w1, w2, offs, away, o
             picked_words[side][1] = gather_words(side, 1)
             for b in range(BLOCKS):
                 product(z_banks[b][side][:], w2_q[1], b, side, 1, slice(0, S), False, True)
+
         w1_first = held.tile([P, N, PACK], BF16, name="w1_first", align_bytes=64)
-        w1_second = reused.tile([P, N, PACK], BF16, name="w1_second", offset=T * 4, align_bytes=64)
+        w1_second = reused.tile([P, N, PACK], BF16, name="w1_second", offset=W1_GROUPED_AT, align_bytes=64)
         w1_grouped = [
             interleave(nc.scalar.copy, w1_raw[0], w1_first),
             interleave(nc.vector.tensor_copy, w1_raw[1], w1_second),
         ]
+
         for side in range(2):
             for b in range(BLOCKS):
                 nc.scalar.activation(
@@ -150,10 +170,11 @@ def tile_picked_yskill_var_p_kernel(tc, x_words, x_scales, w1, w2, offs, away, o
 
         w1_q = []
         for g in range(PASSES):
-            codes = reused.tile([P, N], U32, name=f"w1{g}_codes", offset=T * 4 + 2048 + g * N * 4, align_bytes=64)
+            at = W1_CODES_AT + g * CODE_BYTES
+            codes = reused.tile([P, N], U32, name=f"w1{g}_codes", offset=at, align_bytes=64)
             w1_q.append(quantize(w1_grouped[g], codes, f"w1{g}"))
         y_banks = [psum.tile([P, BLOCKS, TEAMS], F32, name=f"y{side}") for side in range(2)]
-        for side in (1, 0):
+        for side in (LOSERS, WINNERS):
             for b in range(BLOCKS):
                 for g in range(PASSES):
                     for d in range(D):
@@ -174,41 +195,43 @@ def tile_picked_yskill_var_p_kernel(tc, x_words, x_scales, w1, w2, offs, away, o
                 total[:, b, :], spread[b][:].rearrange("p l (v d) -> p v l d", d=D), AXIS.XY, ALU.add
             )
         inv_sc = held.tile([P, BLOCKS, TEAMS], F32, name="inv_sc")
-        nc.scalar.activation(inv_sc[:], total[:], ACT.Abs_reciprocal_sqrt, bias=1.0)
+        for b in range(BLOCKS):
+            nc.scalar.activation(inv_sc[:, b, :], total[:, b, :], ACT.Abs_reciprocal_sqrt, bias=1.0)
 
         lead = held.tile([P, BLOCKS, TEAMS], F32, name="lead")
-        losers_y = spread[BLOCKS - 1][:, 1, 0 : BLOCKS * TEAMS].rearrange("p (b v) -> p b v", b=BLOCKS)
+        losers_y = spread[BLOCKS - 1][:, LOSERS, 0 : BLOCKS * TEAMS].rearrange("p (b v) -> p b v", b=BLOCKS)
         t0 = held.tile([P, BLOCKS, TEAMS], F32, name="t0")
         t0_sq = held.tile([P, BLOCKS, TEAMS], F32, name="t0_sq")
-        pull = held.tile([P, BLOCKS, TEAMS], F32, name="pull")
+        gain_sq = held.tile([P, BLOCKS, TEAMS], F32, name="gain_sq")
         for b in range(BLOCKS):
-            nc.vector.tensor_copy(losers_y[:, b, :], y_banks[1][:, b, :])
+            nc.vector.tensor_copy(losers_y[:, b, :], y_banks[LOSERS][:, b, :])
         for b in range(BLOCKS):
-            nc.vector.tensor_tensor(lead[:, b, :], y_banks[0][:, b, :], losers_y[:, b, :], ALU.subtract)
+            nc.vector.tensor_tensor(lead[:, b, :], y_banks[WINNERS][:, b, :], losers_y[:, b, :], ALU.subtract)
         for b in range(BLOCKS):
             nc.vector.tensor_tensor(t0[:, b, :], lead[:, b, :], inv_sc[:, b, :], ALU.mult)
         for b in range(BLOCKS):
             nc.vector.tensor_tensor(t0_sq[:, b, :], t0[:, b, :], t0[:, b, :], ALU.mult)
-        nc.vector.scalar_tensor_tensor(pull[:], t0[:], 1.0 / GAIN, inv_sc[:], ALU.mult, ALU.mult)
-        coef = []
+        nc.vector.scalar_tensor_tensor(gain_sq[:], inv_sc[:], GAIN * GAIN, inv_sc[:], ALU.mult, ALU.mult)
+
+        factors = []
         for b in range(BLOCKS):
             bend = held.tile([P, TEAMS], F32, name=f"bend{b}")
             nc.scalar.activation(bend[:], t0[:, b, :], ACT.Tanh, scale=0.5 * SLOPE, bias=TANH_SHIFT)
             bell = held.tile([P, TEAMS], F32, name=f"bell{b}")
             nc.scalar.activation(bell[:], t0_sq[:, b, :], ACT.Exp, scale=-0.5)
-            bend_sc = held.tile([P, TEAMS], F32, name=f"bend_sc{b}")
-            nc.vector.scalar_tensor_tensor(bend_sc[:], bend[:], TANH_TOP, inv_sc[:, b, :], ALU.subtract, ALU.mult)
             ratio = held.tile([P, TEAMS], F32, name=f"ratio{b}")
-            nc.vector.tensor_tensor(ratio[:], bend_sc[:], bell[:], ALU.mult)
+            nc.vector.scalar_tensor_tensor(ratio[:], bend[:], TANH_TOP, bell[:], ALU.subtract, ALU.mult)
             gap = held.tile([P, TEAMS], F32, name=f"gap{b}")
-            nc.vector.tensor_tensor(gap[:], pull[:, b, :], ratio[:], ALU.subtract)
+            nc.vector.scalar_tensor_tensor(gap[:], t0[:, b, :], 1.0 / GAIN, ratio[:], ALU.mult, ALU.subtract)
+            weighted = held.tile([P, TEAMS], F32, name=f"weighted{b}")
+            nc.vector.tensor_tensor(weighted[:], ratio[:], gain_sq[:, b, :], ALU.mult)
             factor = held.tile([P, TEAMS], F32, name=f"factor{b}")
-            nc.vector.scalar_tensor_tensor(factor[:], gap[:], GAIN * GAIN, ratio[:], ALU.mult, ALU.mult)
-            coef.append(factor)
+            nc.vector.tensor_tensor(factor[:], gap[:], weighted[:], ALU.mult)
+            factors.append(factor)
 
         for b, j0, j1 in ((0, 0, S), (1, 0, HALF), (1, HALF, S)):
-            s1 = spread[b][:, 0, j0:j1]
-            teams = coef[b][:, j0 // D : j1 // D]
+            s1 = spread[b][:, WINNERS, j0:j1]
+            teams = factors[b][:, j0 // D : j1 // D]
             change = held.tile([P, j1 - j0], F32, name=f"change{b}{j0}")
             nc.vector.tensor_tensor(
                 change[:].rearrange("p (v d) -> p v d", d=D),

import math
from contextlib import ExitStack

import concourse.mybir as mybir

K = 1024
T = 2048
S = 512
D = 4
N = 256
P = 128
PACK = 4
K_PASS = P * PACK
PASSES = K // K_PASS
BLOCKS = N // P
TEAMS = S // D
HALF = S // 2
QUADRANT = 32
SCALE_ROWS = 4
RUN = 4
WINNERS, LOSERS = 0, 1

TABLE_BYTES = T * 4
PICKED_BYTES = S * 4
GROUPED_BYTES = N * PACK * 2
CODE_BYTES = N * 4
PICKED_AT = PASSES * TABLE_BYTES
W2_GROUPED_AT = (PICKED_AT + 2 * PICKED_BYTES, PICKED_AT + PICKED_BYTES // 2)
W1_GROUPED_AT = TABLE_BYTES
W1_CODES_AT = W1_GROUPED_AT + GROUPED_BYTES

F32 = mybir.dt.float32
BF16 = mybir.dt.bfloat16
I32 = mybir.dt.int32
U32 = mybir.dt.uint32
U16 = mybir.dt.uint16
U8 = mybir.dt.uint8
FP8X4 = mybir.dt.float8_e4m3fn_x4
ACT = mybir.ActivationFunctionType
ALU = mybir.AluOpType
AXIS = mybir.AxisListType

FLOPS = 4 * 2 * K * N * S

PDF = 0.3989
SLOPE = 1.702
FLOOR = 0.02
TANH_SHIFT = 0.5 * math.log((1.0 + FLOOR) / FLOOR)
TANH_TOP = 1.0 + 2.0 * FLOOR
GAIN = PDF / (2.0 * FLOOR * (1.0 + FLOOR))


def tile_picked_yskill_var_p_kernel(tc, x_words, x_scales, w1, w2, offs, away, out):
    nc = tc.nc
    with ExitStack() as ctx:
        held = ctx.enter_context(tc.tile_pool(name="held", bufs=1))
        reused = ctx.enter_context(tc.tile_pool(name="reused", bufs=1))
        psum = ctx.enter_context(tc.psum_pool(name="psum", bufs=1))

        lists = []
        for side, src in enumerate((offs, away)):
            offsets = held.tile([P, S // 16], U16, name=f"offsets{side}")
            nc.sync.dma_start(offsets[:], src)
            lists.append(offsets)

        scale_table = held.tile([P, T], U8, name="scale_table", align_bytes=64)
        nc.vector.memset(scale_table[:].bitcast(I32), 0)
        for q in range(P // QUADRANT):
            nc.sync.dma_start(
                out=scale_table[QUADRANT * q : QUADRANT * q + SCALE_ROWS * PASSES, :].bitcast(I32),
                in_=x_scales[:, SCALE_ROWS * q : SCALE_ROWS * (q + 1), :].bitcast(I32),
            )

        def load_words(g):
            table = reused.tile([P, T], I32, name=f"word_table{g}", offset=g * TABLE_BYTES, align_bytes=64)
            nc.sync.dma_start(out=table[:], in_=x_words[g].rearrange("p n t -> p (n t)").bitcast(I32))
            return table

        def load_weight(w, name, g):
            raw = held.tile([P, PACK, N], F32, name=f"{name}_raw{g}", align_bytes=64)
            nc.sync.dma_start(out=raw[:], in_=w[g * K_PASS : (g + 1) * K_PASS, :].rearrange("(p j) n -> p j n", j=PACK))
            return raw

        word_tables = [load_words(0)]
        w2_raw = [load_weight(w2, "w2", g) for g in range(PASSES)]
        word_tables.append(load_words(1))
        w1_raw = [load_weight(w1, "w1", g) for g in range(PASSES)]

        picked_scales = []
        for side in range(2):
            picked = held.tile([P, S], U8, name=f"picked_scales{side}", align_bytes=64)
            nc.vector.tensor_copy(picked[:], scale_table[:].indirect(lists[side][:]))
            dealt = held.tile([P, S], U8, name=f"dealt_scales{side}", align_bytes=64)
            nc.vector.tensor_copy(
                dealt[:].rearrange("p (d v) -> p d v", d=D), picked[:].rearrange("p (v d) -> p d v", d=D)
            )
            picked_scales.append(dealt)

        def gather_words(side, g):
            if g == 0:
                picked = held.tile([P, S], U32, name=f"picked_words{side}{g}", align_bytes=64)
            else:
                at = PICKED_AT + side * PICKED_BYTES
                picked = reused.tile([P, S], U32, name=f"picked_words{side}{g}", offset=at, align_bytes=64)
            nc.vector.tensor_copy(
                picked[:].rearrange("p (d v) -> p v d", d=D), word_tables[g][:].bitcast(U32).indirect(lists[side][:])
            )
            return picked

        def interleave(copy, raw, grouped):
            copy(
                grouped[:].rearrange("p (c i) t -> p c t i", i=RUN),
                raw[:].rearrange("p t (c i) -> p c t i", i=RUN),
            )
            return grouped

        def quantize(grouped, codes, name):
            scales = held.tile([P, N], U8, name=f"{name}_scales", align_bytes=64)
            nc.vector.quantize_mx(
                out=codes[:].bitcast(FP8X4), scales=scales[:], in_=grouped[:].rearrange("p n t -> p (n t)")
            )
            return codes, scales

        def product(bank, quantized, b, side, g, cols, start, stop):
            codes, scales = quantized
            nc.tensor.matmul_mx(
                out=bank,
                lhsT=codes[:, b * P : (b + 1) * P].bitcast(FP8X4),
                lhsT_scale=scales[:, b * P : (b + 1) * P],
                rhs=picked_words[side][g][:, cols].bitcast(FP8X4),
                rhs_scale=picked_scales[side][SCALE_ROWS * g : P, cols],
                start=start,
                stop=stop,
            )

        z_banks = [[psum.tile([P, S], F32, name=f"z{b}{side}") for side in range(2)] for b in range(BLOCKS)]
        picked_words = [[None] * PASSES for side in range(2)]
        spread = [held.tile([P, 2, S], F32, name=f"spread{b}") for b in range(BLOCKS)]

        for side in range(2):
            picked_words[side][0] = gather_words(side, 0)
        w2_q = []
        for g in range(PASSES):
            grouped = reused.tile([P, N, PACK], BF16, name=f"w2{g}_grouped", offset=W2_GROUPED_AT[g], align_bytes=64)
            codes = held.tile([P, N], U32, name=f"w2{g}_codes", align_bytes=64)
            w2_q.append(quantize(interleave(nc.scalar.copy, w2_raw[g], grouped), codes, f"w2{g}"))
        for side in range(2):
            for b in range(BLOCKS):
                product(z_banks[b][side][:], w2_q[0], b, side, 0, slice(0, S), True, False)
        for side in range(2):
            picked_words[side][1] = gather_words(side, 1)
            for b in range(BLOCKS):
                product(z_banks[b][side][:], w2_q[1], b, side, 1, slice(0, S), False, True)

        w1_first = held.tile([P, N, PACK], BF16, name="w1_first", align_bytes=64)
        w1_second = reused.tile([P, N, PACK], BF16, name="w1_second", offset=W1_GROUPED_AT, align_bytes=64)
        w1_grouped = [
            interleave(nc.scalar.copy, w1_raw[0], w1_first),
            interleave(nc.vector.tensor_copy, w1_raw[1], w1_second),
        ]

        for side in range(2):
            for b in range(BLOCKS):
                nc.scalar.activation(
                    spread[b][:, side, :].rearrange("p (v d) -> p v d", d=D),
                    z_banks[b][side][:].rearrange("p (d v) -> p v d", d=D),
                    ACT.Exp,
                    scale=0.5,
                )

        w1_q = []
        for g in range(PASSES):
            at = W1_CODES_AT + g * CODE_BYTES
            codes = reused.tile([P, N], U32, name=f"w1{g}_codes", offset=at, align_bytes=64)
            w1_q.append(quantize(w1_grouped[g], codes, f"w1{g}"))
        y_banks = [psum.tile([P, BLOCKS, TEAMS], F32, name=f"y{side}") for side in range(2)]
        for side in (LOSERS, WINNERS):
            for b in range(BLOCKS):
                for g in range(PASSES):
                    for d in range(D):
                        product(
                            y_banks[side][:, b, :],
                            w1_q[g],
                            b,
                            side,
                            g,
                            slice(d * TEAMS, (d + 1) * TEAMS),
                            g == 0 and d == 0,
                            g == PASSES - 1 and d == D - 1,
                        )

        total = held.tile([P, BLOCKS, TEAMS], F32, name="total")
        for b in range(BLOCKS):
            nc.vector.tensor_reduce(
                total[:, b, :], spread[b][:].rearrange("p l (v d) -> p v l d", d=D), AXIS.XY, ALU.add
            )
        inv_sc = held.tile([P, BLOCKS, TEAMS], F32, name="inv_sc")
        for b in range(BLOCKS):
            nc.scalar.activation(inv_sc[:, b, :], total[:, b, :], ACT.Abs_reciprocal_sqrt, bias=1.0)

        lead = held.tile([P, BLOCKS, TEAMS], F32, name="lead")
        losers_y = spread[BLOCKS - 1][:, LOSERS, 0 : BLOCKS * TEAMS].rearrange("p (b v) -> p b v", b=BLOCKS)
        t0 = held.tile([P, BLOCKS, TEAMS], F32, name="t0")
        t0_sq = held.tile([P, BLOCKS, TEAMS], F32, name="t0_sq")
        gain_sq = held.tile([P, BLOCKS, TEAMS], F32, name="gain_sq")
        for b in range(BLOCKS):
            nc.vector.tensor_copy(losers_y[:, b, :], y_banks[LOSERS][:, b, :])
        for b in range(BLOCKS):
            nc.vector.tensor_tensor(lead[:, b, :], y_banks[WINNERS][:, b, :], losers_y[:, b, :], ALU.subtract)
        for b in range(BLOCKS):
            nc.vector.tensor_tensor(t0[:, b, :], lead[:, b, :], inv_sc[:, b, :], ALU.mult)
        for b in range(BLOCKS):
            nc.vector.tensor_tensor(t0_sq[:, b, :], t0[:, b, :], t0[:, b, :], ALU.mult)
        nc.vector.scalar_tensor_tensor(gain_sq[:], inv_sc[:], GAIN * GAIN, inv_sc[:], ALU.mult, ALU.mult)

        factors = []
        for b in range(BLOCKS):
            bend = held.tile([P, TEAMS], F32, name=f"bend{b}")
            nc.scalar.activation(bend[:], t0[:, b, :], ACT.Tanh, scale=0.5 * SLOPE, bias=TANH_SHIFT)
            bell = held.tile([P, TEAMS], F32, name=f"bell{b}")
            nc.scalar.activation(bell[:], t0_sq[:, b, :], ACT.Exp, scale=-0.5)
            ratio = held.tile([P, TEAMS], F32, name=f"ratio{b}")
            nc.vector.scalar_tensor_tensor(ratio[:], bend[:], TANH_TOP, bell[:], ALU.subtract, ALU.mult)
            gap = held.tile([P, TEAMS], F32, name=f"gap{b}")
            nc.vector.scalar_tensor_tensor(gap[:], t0[:, b, :], 1.0 / GAIN, ratio[:], ALU.mult, ALU.subtract)
            weighted = held.tile([P, TEAMS], F32, name=f"weighted{b}")
            nc.vector.tensor_tensor(weighted[:], ratio[:], gain_sq[:, b, :], ALU.mult)
            factor = held.tile([P, TEAMS], F32, name=f"factor{b}")
            nc.vector.tensor_tensor(factor[:], gap[:], weighted[:], ALU.mult)
            factors.append(factor)

        for b, j0, j1 in ((0, 0, S), (1, 0, HALF), (1, HALF, S)):
            s1 = spread[b][:, WINNERS, j0:j1]
            teams = factors[b][:, j0 // D : j1 // D]
            change = held.tile([P, j1 - j0], F32, name=f"change{b}{j0}")
            nc.vector.tensor_tensor(
                change[:].rearrange("p (v d) -> p v d", d=D),
                s1.rearrange("p (v d) -> p v d", d=D),
                teams.unsqueeze(2).to_broadcast([P, (j1 - j0) // D, D]),
                ALU.mult,
            )
            result = held.tile([P, j1 - j0], F32, name=f"result{b}{j0}")
            nc.vector.scalar_tensor_tensor(result[:], change[:], 1.0, s1, ALU.add, ALU.mult)
            nc.sync.dma_start(out=out[b * P : (b + 1) * P, j0:j1], in_=result[:])
